import numpy as np, ml_dtypes
CORES = [9,25,41,57]
N = 4
BF = ml_dtypes.bfloat16
V, HB, CH, LV, RO = 4096, 1024, 128, 2, 3
def places(w, dd):
    u = np.matmul(np.swapaxes(w, -1, -2), dd) & 4095
    return (((u * u) >> 5) + u) & (HB - 1)
def pattern(rng):
    return np.stack([np.tile(rng.integers(0, 256, a), 16 // a) for a in (int(v) for v in rng.choice(np.array([4, 8, 16]), 8))])
def near(rng, b, n):
    i = (np.arange(16)[:, None] + rng.integers(0, 16, (N, 8, 1, n))) % 16
    v = np.take_along_axis(np.broadcast_to(b[None, :, :, None], (N, 8, 16, n)), i, 2)
    s = rng.integers(1, 25, (N, 8, 1, n))
    return np.clip(v + np.rint(s * (2 * rng.random((N, 8, 16, n)) - 1)).astype(np.int64), 0, 255)
def parts(rng):
    b = pattern(rng); x = near(rng, b, V); x = np.where(rng.random((N, 8, 1, V)) < 0.1, rng.integers(0, 256, x.shape), x); c = near(rng, b, CH)
    h = rng.integers(0, V, (N, 8, 16, HB)); h[rng.random(h.shape) < 0.15] = V
    l = rng.integers(0, V, (N, 8, 16, V)); l[rng.random(l.shape) < 0.25] = V
    return x, h, l, c, rng.integers(0, 256, (8, 16, 16)), rng.integers(80, 400, (N, 8, 16))
def pack(x, h, l, c, w, t):
    return {"xr": np.ascontiguousarray(x.reshape(N, 128, V)).astype(np.float32).astype(BF), "hd": np.ascontiguousarray(h.reshape(N, 128, HB)).astype(np.int32),
            "nx": np.ascontiguousarray(l.reshape(N, 128, V)).astype(np.int32), "c0": np.ascontiguousarray(c.reshape(N, 128, CH)).astype(np.float32).astype(BF),
            "wt": np.tile(w.reshape(1, 128, 16), (N, 1, 1)).astype(np.float32).astype(BF), "th": np.ascontiguousarray(t.reshape(N, 128, 1)).astype(np.int32)}
def setup_inputs(rng):
    return pack(*parts(rng))
def setup_inputs_crowd(rng):
    x, h, l, c, w, t = parts(rng)
    c[:, ::2] = np.take_along_axis(c, rng.integers(0, 5, (N, 8, 1, CH)), 3)[:, ::2]
    few = np.concatenate([np.array([0, V - 1]), 1 + rng.permutation(V - 2)[:30]])
    h[:, 1::2] = rng.choice(few, (N, 4, 16, HB))
    return pack(x, h, l, c, w, t)
def setup_inputs_ties(rng):
    x, h, l, c, w, t = parts(rng)
    t = rng.choice(np.array([0, 1, 15, 16, 17, 100, 250, 400]), (N, 8, 16)); x[:, ::2] = rng.integers(0, 256, (N, 4, 16, V))
    e = rng.integers(0, 2, (N, 2, 16, 1)) == 1; a = rng.integers(0, 16, (N, 2, 16, CH)); b = rng.integers(0, 16, (N, 2, 16, V))
    c[:, 2::4] = np.roll(np.where(e, 255 - a, a), 1, axis=2); x[:, 2::4] = np.where(e, b, 255 - b); t[:, 2::4] = rng.integers(1500, 3501, (N, 2, 16))
    dd = np.roll(c, -1, axis=2); k = places(w[None], dd); cc = np.arange(CH)
    for q in range(N):
        for g in range(8):
            o = rng.permutation(V)[:8 * CH].reshape(CH, 8); ds = np.argsort(rng.random((CH, 16)), axis=1)[:, :8]; hg, lg, xg, dg = h[q, g], l[q, g], x[q, g], dd[q, g]
            for j in range(8):
                d = ds[:, j]; rd = o[:, j]; at = k[q, g][d, cc]
                if j < 4: hg[d, at] = rd
                else:
                    e = hg[d, at]
                    if LV == 3 and j >= 6: e = np.where(e < V, lg[d, np.minimum(e, V - 1)], V)
                    m = e < V; lg[d[m], e[m]] = rd[m]
                far = np.maximum(t[q, g][d] + rng.integers(-1, 2, CH), 0)
                z = np.minimum(rng.integers(0, 9, (16, CH)), (far // 16)[None, :])
                step = (far // 16)[None, :] + (np.argsort(rng.random((16, CH)), axis=0) < (far % 16)[None, :]) + z - np.roll(z, 1, axis=0)
                xg[:, rd] = dg + np.where(dg < 128, 1, -1) * step
    return pack(x, h, l, c, w, t)
def setup_inputs_ends(rng):
    x, h, l, c, w, t = parts(rng); m = V // 2
    h[:, 0, :15] = V
    l[:, 1] = V
    x[:, 2:4, :, :m] = rng.integers(0, 256, (N, 2, 16, m)); h[:, 2:4] = rng.integers(0, m, (N, 2, 16, HB)); l[:, 2:4] = rng.integers(m, V, (N, 2, 16, V)); l[:, 3, :15] = V
    h[:, 4] = rng.choice(np.array([0, V - 1, V]), (N, 16, HB)); h[:, 4, 0] = 0; h[:, 4, 1] = V - 1; l[:, 4, :, 0] = V - 1; l[:, 4, :, V - 1] = 0
    x[:, 4, :, 0] = np.roll(c[:, 4, :, 0], -1, axis=1); x[:, 4, :, V - 1] = np.roll(c[:, 4, :, CH - 1], -1, axis=1)
    h[:, 5] = V
    l[:, 6] = np.arange(V)
    return pack(x, h, l, c, w, t)
def setup_inputs_eager(rng):
    x, h, l, c, w, t = parts(rng)
    x = rng.integers(0, 256, x.shape); c = rng.integers(0, 256, c.shape); t[:] = 4080
    x[:, 0] = 255 * rng.integers(0, 2, (N, 1, V)); c[:, 0] = 255 * rng.integers(0, 2, (N, 1, CH)); t[:, 0] = 4079 + rng.integers(0, 2, (N, 16))
    w[0] = 255; w[1] = 0; w[2] = rng.choice(np.array([0, 1, 255]), (16, 16)); t[:, 3] = 4079
    return pack(x, h, l, c, w, t)
def setup_inputs_spread(rng):
    x, h, l, c, w, t = parts(rng)
    x = np.minimum((np.exp2(8 * rng.random((N, 8, 1, V))) * rng.random((N, 8, 16, V))).astype(np.int64), 255)
    c = np.minimum((np.exp2(8 * rng.random((N, 8, 1, CH))) * rng.random((N, 8, 16, CH))).astype(np.int64), 255)
    w = np.minimum((np.exp2(8 * rng.random((8, 1, 16))) * (0.5 + 0.5 * rng.random((8, 16, 16)))).astype(np.int64), 255)
    t = np.minimum(np.exp2(12 * rng.random((N, 8, 16))).astype(np.int64), 4080)
    p = 1 + 2 * rng.random((N, 8, 16, 1))
    h = np.where(h == V, V, np.minimum((V * rng.random(h.shape) ** p).astype(np.int64), V - 1))
    l = np.where(l == V, V, np.minimum((V * rng.random(l.shape) ** p).astype(np.int64), V - 1))
    return pack(x, h, l, c, w, t)
def check_inputs(d):
    bad = []
    for k, lo, hi in (("xr", 0, 255), ("hd", 0, V), ("nx", 0, V), ("c0", 0, 255), ("wt", 0, 255), ("th", 0, 4080)):
        v = np.asarray(d[k]).astype(np.float64)
        if not bool(np.all((v >= lo) & (v <= hi))): bad.append("range of " + k)
        elif bool(np.any(v != np.floor(v))): bad.append("whole numbers in " + k)
    v = np.asarray(d["wt"]).astype(np.float64)
    if bool(np.any(v != v[:1])): bad.append("wt alike on all ranks")
    return bad
def reference(xr, hd, nx, c0, wt, th):
    x = np.concatenate([xr.astype(np.float32).astype(np.int64).reshape(N, 8, 16, V), np.full((N, 8, 16, 1), 512, np.int64)], axis=3)
    h = hd.astype(np.int64).reshape(N, 8, 16, HB); l = np.concatenate([nx.astype(np.int64).reshape(N, 8, 16, V), np.full((N, 8, 16, 1), V, np.int64)], axis=3)
    c = c0.astype(np.float32).astype(np.int64).reshape(N, 8, 16, CH); w = wt.astype(np.float32).astype(np.int64).reshape(N, 8, 16, 16)
    lim = np.tile(th.astype(np.int64).reshape(N, 8, 16), (1, 1, LV))[..., None]; low = np.tri(CH, k=-1, dtype=bool); took = np.zeros((N, 8, RO, CH), np.int64)
    for t in range(RO):
        dd = np.roll(c, -1, axis=2)
        cand = [np.take_along_axis(h, places(w, dd), 3)]
        for i in range(1, LV): cand.append(np.take_along_axis(l, cand[-1], 3))
        cd = np.concatenate(cand, axis=2)
        v = np.take_along_axis(x, cd.reshape(N, 8, 1, 16 * LV * CH), 3).reshape(N, 8, 16, 16 * LV, CH)
        good = np.add.reduce(np.abs(v - dd[:, :, :, None, :]), axis=2) <= lim
        first = np.argmax(good, axis=2)[:, :, None, :]
        rd = np.where(np.any(good, axis=2), np.take_along_axis(cd, first, 2)[:, :, 0], V)
        lost = np.any((rd[..., :, None] == rd[..., None, :]) & low, axis=-1)
        win = (rd < V) & ~lost; rd = np.where(win, rd, V); took[:, :, t] = rd
        c = np.where(win[:, :, None, :], (3 * dd + np.take_along_axis(x, rd[:, :, None, :], 3)) >> 2, dd)
        np.put_along_axis(x, rd[:, :, None, :], 512, 3)
        c = np.roll(c, 1 + t % (N - 1), axis=0)
    return {"yc": c.reshape(N, 128, CH).astype(np.float32), "yt": took.reshape(N, 8, RO * CH).astype(np.float32)}

@@ -1,0 +1,447 @@
+from concourse.mybir import dt, AluOpType, AxisListType, ActivationFunctionType
+import comms_topo
+
+OP = AluOpType
+AF = ActivationFunctionType
+V, HB, CH, RO, H = 4096, 1024, 128, 3, 64
+XE = V + 8
+XW = XE + 4 * H
+A, B, NCH = 0.05, 5.0, 2
+
+SCRATCH = {"dx": ("psum", [128, 1024], "float32")}
+
+
+def buf(shape, dtype, names, where="sbuf"):
+    for n in names.split():
+        SCRATCH[n] = (where, shape, dtype)
+
+
+buf([128, 512], "float32", "p2 p3 p4 p5 p6 p7", "psum")
+buf([128, XW], "bfloat16", "xs")
+buf([128, HB], "int32", "hdi")
+buf([128, HB], "float32", "hdf mg128")
+buf([128, XE], "int32", "nxs")
+buf([128, 1], "int32", "thi pi pdi")
+COLS = "pc pd pg pg15 corr s0 sc0 scl thf dmo0 dmo1 thr0 thr1 dum0 dum1".split()
+buf([128, 16], "float32", "cols ma mb")
+buf([128, CH], "bfloat16", "cb c512 xrot tri nb2 nbk")
+buf([128, 16], "bfloat16", "wts wt2")
+buf([128, 128], "float32", "m15 mg kt kx blk4 tr1 tr2 blf idf xm0 xm1 dd yo")
+buf([128, 143], "float32", "mf")
+buf([64, 1024], "float32", "ce")
+buf([128, 4], "float32", "sq qm")
+buf([128, 2048], "float32", "seli")
+buf([128, 2048], "float16", "sel")
+buf([128, 128], "float16", "rot wr blh brow cf cca ccb")
+buf([128, 2], "float16", "k4")
+buf([128, 2], "float32", "k4f")
+buf([128, 143], "bfloat16", "bigm")
+buf([64, 64], "float16", "idh")
+buf([64, 128], "float16", "far")
+buf([128, 1024], "float16", "msk")
+buf([64, 1024], "bfloat16", "exp")
+buf([128, 512], "float32", "ms")
+buf([1, 128], "float32", "half zero pow")
+buf([1, 16], "float32", "one")
+buf([128, 24], "float32", "yq")
+buf([16, 128], "float32", "yt1")
+buf([8, 128], "float32", "yt2")
+buf([128, 128], "int32", "ui ua ub up uh ai")
+buf([128, 128], "uint16", "hh ah bh")
+for _h in "01":
+    buf([64, 128], "bfloat16", "dt" + _h)
+    buf([128, 1024], "float32", "gh" + _h + " sn" + _h)
+    buf([128, 1024], "float16", "gn" + _h)
+    buf([128, 128], "bfloat16", "near" + _h + " cho" + _h)
+    buf([128, 512], "bfloat16", "eq" + _h)
+    buf([64, 128], "float32", "win" + _h)
+    buf([128, 1024], "bfloat16", " ".join(k + l + _h for k in ("xg", "yy", "av") for l in "ab"))
+for _t in range(RO):
+    buf([128, 128], "float16", "rdf%d" % _t)
+    buf([128, 8], "uint16", "off%d" % _t)
+    buf([128, H], "float16", " ".join("%s%d%d" % (k, _t, h) for k in ("cn", "cl") for h in range(2)))
+DMAS = ["c0", "wt", "th", "hd", "xr", "nx", "yc0", "yc1"] + ["yt1%d" % k for k in range(8)] + ["yt2%d" % k for k in range(8)]
+SEMAPHORES = ["eV", "eS", "eP", "eG", "sent"] + ["arr%d%d" % (t, h) for t in range(RO) for h in range(2)] + ["d_" + k for k in DMAS]
+
+CY, FX, LAT = 0.00104, 0.06, 0.07
+GA = 1.56
+
+
+def schedule(ops):
+    n = len(ops)
+    succ = [[] for _ in range(n)]
+    for o in ops:
+        for d in o["deps"]:
+            succ[d].append(o["id"])
+    prio = [0.0] * n
+    for k in range(n - 1, -1, -1):
+        prio[k] = ops[k]["dur"] + ops[k]["lat"] + max([prio[s] + LAT for s in succ[k]] or [0.0])
+    want = [prio[k] - B * ops[k]["st"] for k in range(n)]
+    left = [len(o["deps"]) for o in ops]
+    ready = {}
+    for k in range(n):
+        if left[k] == 0:
+            ready.setdefault(ops[k]["eng"], []).append(k)
+    fin, free, bank, order, begin = [0.0] * n, {}, {}, [], [0.0] * n
+    while any(ready.values()):
+        pick = None
+        for e in ready:
+            est = []
+            for k in ready[e]:
+                o = ops[k]
+                s = max([free.get(e, 0.0) if e else 0.0] + [fin[d] + LAT for d in o["deps"]])
+                for b in o["banks"]:
+                    for x, q in bank.get(b, {}).items():
+                        if x != e:
+                            s = max(s, fin[q] + LAT)
+                est.append((s, k))
+            if est:
+                t = min(est)[0]
+                if pick is None or t < pick[0]:
+                    w, k, s = max((want[k], -k, s) for s, k in est if s <= t + A)
+                    pick = (t, -k, s)
+        t, k, s = pick
+        o = ops[k]
+        e = o["eng"]
+        ready[e].remove(k)
+        begin[k] = s
+        fin[k] = s + o["dur"] + o["lat"]
+        if e:
+            free[e] = s + o["dur"]
+        for b in o["banks"]:
+            q = bank.setdefault(b, {})
+            o["bdeps"] += [v for x, v in q.items() if x != e]
+            q[e] = k
+        order.append(k)
+        for x in succ[k]:
+            left[x] -= 1
+            if left[x] == 0:
+                ready.setdefault(ops[x]["eng"], []).append(x)
+    return order, begin, fin
+
+
+def declare(g, core, T, topo):
+    rank = T.rank_of(core)
+    ops, lastw, readers, stage = [], {}, {}, [0]
+
+    def op(eng, dur, rd, wr, fn, banks=(), sem=None, lat=0.0, name="", strict=False):
+        k = len(ops)
+        deps, war = set(), set()
+        for r in rd + wr:
+            if r in lastw:
+                deps.add(lastw[r])
+        for w in wr:
+            for q in readers.get(w, []):
+                if ops[q]["eng"] == eng and not ops[q]["sem"] and q not in deps and not strict:
+                    war.add(q)
+        for w in wr:
+            deps |= set(readers.get(w, []))
+        for r in rd:
+            readers.setdefault(r, []).append(k)
+        for w in wr:
+            lastw[w] = k
+            readers[w] = []
+        deps.discard(k)
+        ops.append({"id": k, "eng": eng, "dur": dur, "lat": lat, "deps": sorted(deps), "bdeps": [], "war": war, "fn": fn,
+                    "banks": tuple(banks), "sem": sem, "name": name or wr[0], "st": stage[0]})
+
+    def vd(n, c=1.0):
+        return FX + max(64, n * c) * CY
+
+    def S(n):
+        return T[n]
+
+    def co(n, a=0, b=128):
+        j = COLS.index(n)
+        return T.cols[a:b, j:j + 1]
+
+    def ts(out, okey, in0, rd, s1, op0, n, s2=None, op1=None, c=1.0, banks=()):
+        def fn():
+            if op1 is None:
+                return g.vector.tensor_scalar(out, in0, s1, None, op0)
+            return g.vector.tensor_scalar(out, in0, s1, s2, op0, op1)
+        op("V", vd(n, c), rd, [okey], fn, banks)
+
+    def tt(out, okey, in0, in1, rd, o, n, c=2.0, banks=()):
+        op("V", vd(n, c), rd, [okey], lambda: g.vector.tensor_tensor(out, in0, in1, o), banks)
+
+    def cp(out, okey, in_, rd, n, banks=()):
+        op("V", vd(n), rd, [okey], lambda: g.vector.tensor_copy(out, in_), banks)
+
+    def ms(ap, key, val, n):
+        op("V", vd(n), [], [key], lambda: g.vector.memset(ap, val))
+
+    def act(out, okey, in_, rd, n, func, c=1.0, banks=(), **kw):
+        op("S", vd(n, c), rd, [okey], lambda: g.scalar.activation(out, in_, func, **kw), banks)
+
+    def io(ap, key, pattern, base, cm, n):
+        op("G", 0.16 + 2 * n * CY, [], [key], lambda: g.iota(ap, pattern, base, cm, allow_small_or_imprecise_dtypes=True))
+
+    def mm(calls, rd, wr, banks, cyc):
+        def fn():
+            for out, l, r, a, z in calls:
+                q = g.tensor.matmul(out, l, r, a, z)
+            return q
+        op("P", 0.03 + cyc * CY, rd, [wr], fn, banks)
+
+    def mc(calls, rd, wr, banks, cyc):
+        w = len(calls) // NCH
+        for j in range(NCH):
+            mm(calls[j * w:j * w + w], rd, wr, banks, cyc / NCH)
+            if j:
+                ops[-1]["war"].add(ops[-2]["id"])
+
+    def dma(eng, out, in_, rd, wr, sem, lat):
+        q = g.sync if eng == "Y" else g.scalar
+        op(eng, 0.1, rd, [wr], lambda: q.dma_start(out, in_), sem=("d_" + sem, 16), lat=lat)
+
+    dma("Y", T.cb[:], T.c0[:], [], "cb", "c0", 2.0)
+    dma("S", T.wts[:], T.wt[:], [], "wts", "wt", 2.0)
+    dma("Y", T.hdi[:], T.hd[:], [], "hdi", "hd", 4.0)
+    dma("S", T.thi[:], T.th[:], [], "thi", "th", 2.0)
+    dma("Y", T.xs[:, 0:V], T.xr[:], [], "x", "xr", 7.0)
+    dma("Y", T.nxs[:, 0:V], T.nx[:], [], "nx", "nx", 12.0)
+    io(co("pc"), "pc", [[0, 1]], 0, 1, 1)
+    op("G", 0.16, [], ["pi"], lambda: g.iota(T.pi[:], [[0, 1]], 0, 1))
+
+    def iwrap(b, key, base, col, wbase):
+        io(b[:], key, [[16, 8], [1, 16]], base, 0, 128)
+        op("G", 0.18, [key], [key], lambda: g.iota(b[:, col:128:16], [[16, 8]], wbase, 0, allow_small_or_imprecise_dtypes=True))
+    iwrap(T.kx, "kx", -1, 0, 15)
+    io(T.mg[:], "mg", [[16, 8], [0, 16]], 0, 0, 128)
+    iwrap(T.kt, "kt", 1, 15, 0)
+    io(T.m15[:], "m15", [[0, 8], [1, 16]], 0, 0, 128)
+    io(T.mf[:], "mf", [[1, 143]], 0, 0, 143)
+    io(T.ce[:], "ce", [[1, 64], [0, 16]], 0, 0, 1024)
+    io(T.seli[:], "seli", [[4096, 16], [16, 8], [-4095, 16]], 0, 0, 2048)
+    io(T.mg128[:], "mg128", [[16, 8], [0, 128]], 0, 0, 1024)
+    io(T.sq[:], "sq", [[16, 4]], 0, 0, 4)
+    pc, pd, pg = co("pc"), co("pd"), co("pg")
+    ts(T.xrot[:], "xrot", T.kx[:], ["kx", "pc"], pc, OP.is_equal, 128)
+    ts(T.pdi[:], "pdi", T.pi[:], ["pi"], 15, OP.bitwise_and, 1)
+    cp(pd, "pd", T.pdi[:], ["pdi"], 1)
+    tt(pg, "pg", pc, pd, ["pc", "pd"], OP.subtract, 1)
+    ts(T.blk4[:], "blk4", T.mg[:], ["mg", "pg"], pg, OP.is_equal, 128, 0.25, OP.mult)
+    for h in range(2):
+        q = slice(h * H, h * H + H)
+        ts(T.cf[:, q], "cf%d" % h, T.cb[:, q], ["cb"], 4.0, OP.mult, 64, 5120.0, OP.add)
+    mm([(T.p2[:, 384 + 16 * k:400 + 16 * k], T.xrot[:], T.wts[:], True, True) for k in range(8)], ["xrot", "wts"], "RA", ["p2"], 512)
+    tt(T.wr[:], "wr", T.p2[:, 384:512], T.blk4[:], ["RA", "blk4"], OP.mult, 128, 1.0, ["p2"])
+    ms(T.k4f[:], "k4f", 5120.0, 2)
+    cp(T.k4[:], "k4", T.k4f[:], ["k4f"], 2)
+    mm([(T.p2[:, 384:386], T.wr[:], T.k4[:], True, True)], ["wr", "k4"], "RA", ["p2"], 64)
+    cp(co("corr"), "corr", T.p2[:, 384:385], ["RA"], 1, ["p2"])
+    ts(T.hdf[:], "hdf", T.hdi[:], ["hdi"], -2048.0, OP.add, 1024)
+    ts(T.rot[:], "rot", T.kt[:], ["kt", "pc"], pc, OP.is_equal, 128, 0.25, OP.mult)
+    ts(T.ma[:], "ma", T.m15[:, 0:16], ["m15", "pd"], pd, OP.is_ge, 16)
+    ts(T.mb[:], "mb", T.m15[:, 0:16], ["m15", "pd"], pd, OP.is_equal, 16, 65535.0, OP.mult)
+    tt(T.ms[:, 0:16], "ms", T.ma[:], T.mb[:], ["ma", "mb"], OP.add, 16)
+    ts(co("s0"), "s0", pd, ["pd"], 0.0, OP.is_gt, 1, 2.0 ** -40, OP.max)
+    tt(T.ms[:, 15:16], "ms", T.ms[:, 15:16], co("s0"), ["ms", "s0"], OP.mult, 1)
+    w = 16
+    while w < 512:
+        act(T.ms[:, w:2 * w], "ms", T.ms[:, 0:w], ["ms"], w, AF.Copy)
+        w *= 2
+    ts(co("sc0"), "sc0", pd, ["pd"], 0.0, OP.is_equal, 1, 2.0 ** 24, OP.mult)
+    ts(co("scl"), "scl", co("sc0"), ["sc0"], 2.0 ** -16, OP.max, 1)
+    ts(T.exp[:], "exp", T.ce[:], ["ce", "pc"], co("pc", 0, 64), OP.is_equal, 1024)
+    ts(co("pg15"), "pg15", pg, ["pg"], 15.0, OP.add, 1)
+    ts(T.bigm[:], "bigm", T.mf[:], ["mf", "pg15"], co("pg15"), OP.is_equal, 143)
+    ts(T.sel[:], "sel", T.seli[:], ["seli", "pc"], pc, OP.is_equal, 2048)
+    ms(T.nxs[:, V:XE], "nxe", 4096, 8)
+    ms(T.xs[:, V:XE], "xe", 512.0, 8)
+    ms(T.c512[:], "c512", 512.0, 128)
+    cp(co("thf"), "thf", T.thi[:], ["thi"], 1)
+    mf = T.mf[:, 0:128]
+    ts(T.blf[:], "blf", T.mg[:], ["mg", "pg"], pg, OP.is_equal, 128)
+    ts(T.tr1[:], "tr1", mf, ["mf", "pc"], pc, OP.is_gt, 128, -2.0, OP.mult)
+    tt(T.tr2[:], "tr2", T.tr1[:], T.blf[:], ["tr1", "blf"], OP.mult, 128)
+    ts(T.idf[:], "idf", mf, ["mf", "pc"], pc, OP.is_equal, 128)
+    tt(T.tri[:], "tri", T.tr2[:], T.idf[:], ["tr2", "idf"], OP.add, 128)
+    ts(T.nb2[:], "nb2", T.blf[:], ["blf"], -2.0, OP.mult, 128)
+    ts(T.nbk[:], "nbk", T.blf[:], ["blf"], -4096.0, OP.mult, 128)
+    cp(T.blh[:], "blh", T.blf[:], ["blf"], 128)
+    ts(T.msk[:], "msk", T.mg128[:], ["mg128", "pc"], pc, OP.is_equal, 1024)
+    ts(T.brow[:], "brow", T.mg[:], ["mg", "pc"], pc, OP.is_equal, 128)
+    cp(T.idh[:], "idh", T.idf[0:64, 0:64], ["idf"], 64)
+    ts(T.far[:], "far", T.m15[0:64, :], ["m15", "pd"], co("pd", 0, 64), OP.not_equal, 128, 16384.0, OP.mult)
+    ts(T.qm[0:64, :], "qm0", T.sq[0:64, :], ["sq", "pg"], co("pg", 0, 64), OP.is_equal, 4)
+    ts(T.qm[64:128, :], "qm1", T.sq[64:128, :], ["sq", "pg"], 64.0, OP.add, 4, co("pg", 64, 128), OP.is_equal)
+    ms(T.half[:], "half", 0.5, 128)
+    ms(T.zero[:], "zero", 0.0, 128)
+    ms(T.one[:], "one", 1.0, 16)
+    op("V", vd(128), ["half", "zero"], ["pow"], lambda: g.vector.tensor_tensor_scan(T.pow[:], T.half[:], T.zero[:], 2.0 ** 64, OP.mult, OP.add))
+    mm([(T.p7[:, 0:16], T.pow[:], T.one[:], True, True)], ["pow", "one"], "R0", ["p7"], 256)
+    cp(T.wt2[:], "wt2", T.p7[:, 0:16], ["R0"], 16, ["p7"])
+    ts(co("thr0", 0, 64), "thr0", T.p7[0:64, 0:1], ["R0"], 2.5, OP.mult, 1, banks=["p7"])
+    ts(co("thr1", 0, 64), "thr1", co("thr0", 0, 64), ["thr0"], 2.0 ** -64, OP.mult, 1)
+    for h in range(2):
+        dum, dmo = "dum%d" % h, "dmo%d" % h
+        ts(co(dum, 0, 64), dum, co("pc", 0, 64), ["pc"], 2.0, OP.mult, 1, float(XE - 2048 + 2 * H * h), OP.add)
+        ts(co(dmo), dmo, pc, ["pc"], 2.0, OP.mult, 1, float(XE + 2 * H * h - 128), OP.add)
+        ts(S("xm%d" % h)[64:128, :], "xmc%d" % h, T.m15[64:128, :], ["m15", "pd", dmo], co("pd", 64, 128), OP.is_equal, 128,
+           co(dmo, 64, 128), OP.mult)
+
+    for t in range(RO):
+        offk, rdk = "off%d" % t, "rdf%d" % t
+        off, rdf = S(offk), S(rdk)
+        for h in range(2):
+            hs = str(h)
+            hq = slice(h * H, h * H + H)
+            stage[0] = 2 * t + h
+            ck = "cf" + hs if t == 0 else "cl%d%s" % (t - 1, hs)
+
+            def chain():
+                return T.cf[:, hq] if t == 0 else S(ck)[:]
+            mm([(T.p2[:, hq], T.wr[:], chain(), True, True)], ["wr", ck], "U" + hs, ["p2"], 64)
+            mm([(T.p3[:, 0:64], T.rot[:], chain(), True, True)], ["rot", ck], "D", ["p3"], 64)
+            mm([(T.p3[0:64, 128:256], chain(), T.rot[:], True, True)], ["rot", ck], "DT", ["p3"], 128)
+            ts(T.ui[:, hq], "ui" + hs, T.p2[:, hq], ["U" + hs, "corr"], co("corr"), OP.subtract, 64, banks=["p2"])
+            ts(T.ua[:, hq], "ua" + hs, T.ui[:, hq], ["ui" + hs], 4095, OP.bitwise_and, 64)
+            ts(T.ub[:, hq], "ub" + hs, T.ua[:, hq], ["ua" + hs], 32.0, OP.add, 64)
+            tt(T.up[:, hq], "up" + hs, T.ua[:, hq], T.ub[:, hq], ["ua" + hs, "ub" + hs], OP.mult, 64)
+            ts(T.uh[:, hq], "uh" + hs, T.up[:, hq], ["up" + hs], 5, OP.logical_shift_right, 64, 1023, OP.bitwise_and)
+            cp(T.hh[:, hq], "hh" + hs, T.uh[:, hq], ["uh" + hs], 64)
+            act(S("dt" + hs)[:], "dt" + hs, T.p3[0:64, 128:256], ["DT"], 128, AF.Identity, banks=["p3"], bias=-1280.0)
+            act(T.dd[:, hq], "dd" + hs, T.p3[:, 0:64], ["D"], 64, AF.Identity, banks=["p3"], bias=1278.5, scale=3.0)
+            lo = XE + 2 * H * h
+            act(T.xs[:, lo:lo + 2 * H:2], "xd" + hs, T.p3[:, 0:64], ["D"], 64, AF.Identity, banks=["p3"], bias=-1280.0)
+            for p in range(2):
+                q = slice(p * 512, p * 512 + 512)
+                mm([(T.dx[:, q], S("dt" + hs)[:], T.exp[:, q], True, True)], ["dt" + hs, "exp"], "DX%d" % p, ["x%d" % p], 512)
+            gh, sn = S("gh" + hs), S("sn" + hs)
+            for p in range(2):
+                q, ps, lq = slice(p * 512, p * 512 + 512), hs + "p%d" % p, slice(h * H + p * 32, h * H + p * 32 + 32)
+                act(gh[:, q], "gh" + ps, T.hdf[:].indirect(T.hh[:, lq]), ["hdf", "hh" + hs], 512, AF.Copy, c=GA)
+                op("V", vd(512), ["gh" + ps, "ms"], ["sn" + ps],
+                   lambda gh=gh, sn=sn, q=q: g.vector.tensor_tensor_scan(sn[:, q], gh[:, q], T.ms[:], 0.0, OP.add, OP.mult))
+            ts(T.ai[:, hq], "ai" + hs, sn[:, 15:1024:16], ["sn" + hs + "p0", "sn" + hs + "p1", "scl"], co("scl"), OP.mult, 64)
+            ts(T.ah[:, hq], "ah" + hs, T.ai[:, hq], ["ai" + hs], 2048.0, OP.add, 64)
+            gn = S("gn" + hs)
+            ts(gn[:], "gn" + hs, T.nxs[:].indirect(T.ah[:, hq]), ["nx", "nxe", "ah" + hs], 2048.0, OP.subtract, 1024, c=GA)
+            mc([(T.p4[:, hq], T.sel[:, d * 128:d * 128 + 128], gn[:, d:1024:16], d == 0, d == 15) for d in range(16)],
+               ["sel", "gn" + hs], "B" + hs, ["p4"], 1024)
+            ts(T.bh[:, hq], "bh" + hs, T.p4[:, hq], ["B" + hs], 2048.0, OP.add, 64, banks=["p4"])
+            for l, lv in enumerate("ab"):
+                xg, yy, av = S("xg" + lv + hs), S("yy" + lv + hs), S("av" + lv + hs)
+                for p in range(2):
+                    q, ps, lq = slice(p * 512, p * 512 + 512), lv + hs + "p%d" % p, slice(h * H + p * 32, h * H + p * 32 + 32)
+                    act(xg[:, q], "xg" + ps, T.xs[:, 0:XE].indirect(S(lv + "h")[:, lq]), ["x", "xe", lv + "h" + hs], 512, AF.Copy, c=GA)
+                    tt(yy[:, q], "yy" + ps, xg[:, q], T.dx[:, q], ["xg" + ps, "DX%d" % p], OP.subtract, 512, 1.0, ["x%d" % p])
+                    act(av[:, q], "av" + ps, yy[:, q], ["yy" + ps], 512, AF.Abs)
+                z = h * 128 + l * 64
+                mc([(T.p5[:, z:z + 64], T.bigm[:, 15 - d:143 - d], av[:, d:1024:16], d == 0, d == 15)
+                    for d in range(16)], ["bigm", "av" + lv + hs + "p0", "av" + lv + hs + "p1"], "SD" + lv + hs, ["p5"], 1024)
+            nr, cho = S("near" + hs), S("cho" + hs)
+            ts(nr[:], "near" + hs, T.p5[:, h * 128:h * 128 + 128], ["SDa" + hs, "SDb" + hs, "thf"], co("thf"), OP.is_le, 128, banks=["p5"])
+            z = 256 + h * 128
+            mm([(T.p3[:, z:z + 64], T.tri[:], nr[:, 0:64], True, True), (T.p3[:, z + 64:z + 128], T.tri[:], nr[:, 64:128], True, False),
+                (T.p3[:, z + 64:z + 128], T.nb2[:], nr[:, 0:64], False, True)], ["tri", "nb2", "near" + hs], "Z" + hs, ["p3"], 192)
+            act(cho[:], "cho" + hs, T.p3[:, z:z + 128], ["Z" + hs], 128, AF.Relu, banks=["p3"])
+            tt(T.cca[:, hq], "cca" + hs, cho[:, 0:64], T.ai[:, hq], ["cho" + hs, "ai" + hs], OP.mult, 64)
+            tt(T.ccb[:, hq], "ccb" + hs, cho[:, 64:128], T.p4[:, hq], ["cho" + hs, "B" + hs], OP.mult, 64, 1.0, ["p4"])
+            rb = T.p6[:, hq]
+            mm([(rb, T.nbk[:], cho[:, 0:64], True, False), (rb, T.nbk[:], cho[:, 64:128], False, False),
+                (rb, T.blh[:], T.cca[:, hq], False, False), (rb, T.blh[:], T.ccb[:, hq], False, True)],
+               ["nbk", "blh", "cho" + hs, "cca" + hs, "ccb" + hs], "RB" + hs, ["p6"], 256)
+            ts(rdf[:, hq], rdk + hs, rb, ["RB" + hs], 4096.0, OP.add, 64, banks=["p6"])
+            m = 64 * (h + 1)
+            low = [rdk + "0", rdk + "1"][:h + 1]
+            mm([(T.p6[0:m, 256:384], rdf[:, 0:m], T.brow[:], True, True)], ["brow"] + low, "RC", ["p6"], 128)
+            eq = S("eq" + hs)
+            for b in range(2):
+                mm([(T.p7[0:m, j * 64:j * 64 + 64], T.msk[:, j * 128:j * 128 + m], rdf[:, hq], True, True) for j in range(4 * b, 4 * b + 4)],
+                   ["msk", rdk + hs], "R%d" % b, ["p7"], 256)
+            rt = T.p6[0:64, 384:512]
+            mm([(rt, rdf[:, hq], T.brow[:], True, False), (rt, T.idh[:], T.far[:], False, True)], [rdk + hs, "brow", "idh", "far"],
+               "RT", ["p6"], 256)
+            for b in range(2):
+                for j in range(4 * b, 4 * b + 4):
+                    ts(eq[0:m, j * 64:j * 64 + 64], "eq%s%d" % (hs, j), T.p7[0:m, j * 64:j * 64 + 64], ["R%d" % b, "RC"],
+                       T.p6[0:m, 256 + 16 * j:257 + 16 * j], OP.is_equal, 64, banks=["p7", "p6"])
+                mm([(T.p2[0:64, 128 + 16 * j:144 + 16 * j], eq[0:m, j * 64:j * 64 + 64], T.wt2[0:m, :], True, True) for j in range(4 * b, 4 * b + 4)],
+                   ["eq%s%d" % (hs, j) for j in range(4 * b, 4 * b + 4)] + ["wt2"], "L%d" % b, ["p2"], 256)
+            ts(rt, "RT", rt, ["RT", "dum" + hs], co("dum" + hs, 0, 64), OP.subtract, 128, 0.0, OP.min, banks=["p6"])
+            ts(S("win" + hs)[:], "win" + hs, T.p2[0:64, 128:256], ["L0", "L1", "thr" + hs], co("thr" + hs, 0, 64), OP.is_lt, 128, banks=["p2"])
+            xm = S("xm" + hs)
+            tt(xm[0:64, :], "xm" + hs, S("win" + hs)[:], rt, ["win" + hs, "RT"], OP.mult, 128, 1.0, ["p6"])
+            o4 = T.p4[:, 128 + 4 * h:132 + 4 * h]
+            mm([(o4, xm[:], T.qm[:], True, True)], ["xm" + hs, "xmc" + hs, "qm0", "qm1"], "O" + hs, ["p4"], 256)
+            cp(off[:, h * 4:h * 4 + 4], offk + hs, o4, ["O" + hs], 4, ["p4"])
+            cn, cl = "cn%d%s" % (t, hs), "cl%d%s" % (t, hs)
+            tt(S(cn)[:], cn, T.xs[:].indirect(off[:, h * 4:h * 4 + 4]), T.dd[:, hq],
+               ["x", "xe", "xd0", "xd1", offk + hs, "dd" + hs], OP.add, 64, GA)
+            dst = T.cores[(rank + 1 + t % 3) % 4]
+
+            def send(dst=dst, cn=cn, cl=cl, t=t, h=h):
+                rid, pid = topo.addr(dst)[0:2]
+                g.remote_dma(out_ap=S(cl)[:], in_ap=S(cn)[:], remote_sem=T.sem["arr%d%d" % (t, h)], local_sem=T.sem.sent,
+                             pid=pid, routing_id=rid, dma_engine_mask=topo.mask(core, dst))
+            op("G", 0.3, [cn], ["snd" + cl], send, sem=("none", 0), name="send" + cl)
+            op(None, 0.0, ["snd" + cl], [cl], None, sem=("arr%d%d" % (t, h), len(topo.engines(core, dst))), lat=2.8, name="recv" + cl)
+            yk = (t * 2 + h) * 4
+            act(T.yq[:, yk:yk + 4], "yq%d" % (t // 2), o4, ["O" + hs], 4, AF.Copy, banks=["p4"])
+            if h == 1 and t < RO - 1:
+                op("V", FX + 128 * 3.5 * CY, [offk + "0", offk + "1", "c512"], ["x", "xe", "xd0", "xd1"],
+                   lambda off=off: g.vector.tensor_copy(T.xs[:].indirect(off[:, 0:8]), T.c512[:]), name="scatter", strict=True)
+            if t == RO - 1:
+                ts(T.yo[:, hq], "yo" + hs, S(cl)[:], [cl], 0.25, OP.mult, 64, -1280.0, OP.add)
+                dma("Y", T.yc[:, hq], T.yo[:, hq], ["yo" + hs], "out" + hs, "yc%d" % h, 2.0)
+        if t >= 1:
+            e = t - 1
+            n0, nc = (0, 16) if e == 0 else (16, 8)
+            yb = S("yt%d" % (e + 1))
+            py = T.p6[0:nc, 128:256]
+            op("P", 0.03 + 512 * CY, ["yq%d" % e, "idf"], ["PY"], lambda py=py, n0=n0, nc=nc: g.tensor.transpose(py, T.yq[:, n0:n0 + nc], T.idf[:]), ["p6"])
+            ts(yb[:], "ytb%d" % e, py, ["PY"], 4096.0, OP.min, 128, banks=["p6"])
+            for k in range(8):
+                dma("Y", T.yt[k:k + 1, n0 * 16:(n0 + nc) * 16], yb[:, 16 * k:16 * k + 16], ["ytb%d" % e], "yt%d%d" % (e, k), "yt%d%d" % (e + 1, k), 2.0)
+    return ops
+
+
+def rank_program(g, core, T, topo):
+    if T.rank_of(core) is None:
+        return
+    ops = declare(g, core, T, topo)
+    order = schedule(ops)[0]
+    queue = {"V": g.vector, "S": g.scalar, "P": g.tensor, "G": g, "Y": g.sync}
+    count = {"V": 0, "S": 0, "P": 0, "G": 0}
+    known = {e: {} for e in queue}
+    done = [None] * len(ops)
+    for k in order:
+        o = ops[k]
+        e = o["eng"]
+        if e is None:
+            done[k] = (o["sem"][0], o["sem"][1], {})
+            continue
+        need = {}
+        for d in (set(o["deps"]) - o["war"]) | set(o["bdeps"]):
+            s, v, kn = done[d]
+            if s == "none":
+                continue
+            if known[e].get(s, 0) < v and (s not in need or need[s][0] < v):
+                need[s] = (v, kn)
+        for s in sorted(need):
+            if not any(q != s and need[q][1].get(s, 0) >= need[s][0] for q in need):
+                queue[e].wait_ge(T.sem[s], need[s][0])
+        for s in need:
+            v, kn = need[s]
+            known[e][s] = max(known[e].get(s, 0), v)
+            for q, x in kn.items():
+                known[e][q] = max(known[e].get(q, 0), x)
+        ins = o["fn"]()
+        if o["sem"] is None:
+            count[e] += 1
+            ins.then_inc(T.sem["e" + e], 1)
+            done[k] = ("e" + e, count[e], dict(known[e]))
+        elif o["sem"][0] == "none":
+            done[k] = ("none", 0, {})
+        else:
+            ins.then_inc(T.sem[o["sem"][0]], o["sem"][1])
+            done[k] = (o["sem"][0], o["sem"][1], dict(known[e]))
+    g.wait_ge(T.sem.sent, sum(o["sem"][1] for o in ops if o["eng"] is None))
+    for e in sorted(count):
+        g.wait_ge(T.sem["e" + e], count[e])
+    for s in DMAS:
+        if s[0] == "y":
+            g.sync.wait_ge(T.sem["d_" + s], 16)

@@ -6,7 +6,12 @@ AF = ActivationFunctionType
 V, HB, CH, RO, H = 4096, 1024, 128, 3, 64
 XE = V + 8
 XW = XE + 4 * H
-A, B, NCH = 0.05, 5.0, 2
+A, B, NCH = 0.05, 6.0, 2
+LH, LX, LN, CL = 3.3, 10.5, 8.0, 2.8
+PR = {'gh0p0': 2, 'yya1p1': -4, 'sn1p1': 4, 'avb0p0': -2, 'hh0': 8, 'RT0': -8, 'idf0': 14, 'half0': -4, 'ai1': -8, 'dum0': -8,
+      'qm0': -4, 'yo0': -8, 'xgb1p1': -2, 'xm1': -8, 'ua0': 4, 'hh1': 2, 'yyb1p1': 8, 'nb0': -2, 'SDb1': 4, 'ua1': 4, 'blh0': -2,
+      'ah1': -2, 'ui0': 2, 'xga0p0': 8, 'pdi0': -4, 'nbk0': -8, 'ah0': -2, 'ms0': 8, 'one0': -8, 'U1': -8, 'ma0': -4, 'xe0': 2,
+      'bh1': 14}
 
 SCRATCH = {"dx": ("psum", [128, 1024], "float32")}
 
@@ -23,15 +28,14 @@ buf([128, HB], "float32", "hdf mg128")
 buf([128, XE], "int32", "nxs")
 buf([128, 1], "int32", "thi pi pdi")
 COLS = "pc pd pg pg15 corr s0 sc0 scl thf dmo0 dmo1 thr0 thr1 dum0 dum1".split()
-buf([128, 16], "float32", "cols ma mb")
+buf([128, 16], "float32", "cols ma mb eqd")
 buf([128, CH], "bfloat16", "cb c512 xrot tri nb2 nbk")
 buf([128, 16], "bfloat16", "wts wt2")
 buf([128, 128], "float32", "m15 mg kt kx blk4 tr1 tr2 blf idf xm0 xm1 dd yo")
 buf([128, 143], "float32", "mf")
 buf([64, 1024], "float32", "ce")
 buf([128, 4], "float32", "sq qm")
-buf([128, 2048], "float32", "seli")
-buf([128, 2048], "float16", "sel")
+buf([128, 2048], "bfloat16", "sel")
 buf([128, 128], "float16", "rot wr blh brow cf cca ccb")
 buf([128, 2], "float16", "k4")
 buf([128, 2], "float32", "k4f")
@@ -63,7 +67,7 @@ for _t in range(RO):
 DMAS = ["c0", "wt", "th", "hd", "xr", "nx", "yc0", "yc1"] + ["yt1%d" % k for k in range(8)] + ["yt2%d" % k for k in range(8)]
 SEMAPHORES = ["eV", "eS", "eP", "eG", "sent"] + ["arr%d%d" % (t, h) for t in range(RO) for h in range(2)] + ["d_" + k for k in DMAS]
 
-CY, FX, LAT = 0.00104, 0.06, 0.07
+CY, FX, LAT = 0.00095, 0.03, 0.03
 GA = 1.56
 
 
@@ -77,6 +81,11 @@ def schedule(ops):
     for k in range(n - 1, -1, -1):
         prio[k] = ops[k]["dur"] + ops[k]["lat"] + max([prio[s] + LAT for s in succ[k]] or [0.0])
     want = [prio[k] - B * ops[k]["st"] for k in range(n)]
+    for k in range(n):
+        if ops[k]["set"] and (ops[k]["eng"] == "G" or ops[k]["sem"]):
+            want[k] = 1000.0 - k
+        else:
+            want[k] += PR.get(ops[k]["kind"], 0.0)
     left = [len(o["deps"]) for o in ops]
     ready = {}
     for k in range(n):
@@ -122,7 +131,7 @@ def schedule(ops):
 
 def declare(g, core, T, topo):
     rank = T.rank_of(core)
-    ops, lastw, readers, stage = [], {}, {}, [0]
+    ops, lastw, readers, stage, setup = [], {}, {}, [0], [True]
 
     def op(eng, dur, rd, wr, fn, banks=(), sem=None, lat=0.0, name="", strict=False):
         k = len(ops)
@@ -142,8 +151,10 @@ def declare(g, core, T, topo):
             lastw[w] = k
             readers[w] = []
         deps.discard(k)
+        name = name or wr[0]
         ops.append({"id": k, "eng": eng, "dur": dur, "lat": lat, "deps": sorted(deps), "bdeps": [], "war": war, "fn": fn,
-                    "banks": tuple(banks), "sem": sem, "name": name or wr[0], "st": stage[0]})
+                    "banks": tuple(banks), "sem": sem, "name": name, "st": stage[0], "set": setup[0],
+                    "kind": name.strip("0123456789") + str(stage[0] % 2)})
 
     def vd(n, c=1.0):
         return FX + max(64, n * c) * CY
@@ -197,10 +208,10 @@ def declare(g, core, T, topo):
 
     dma("Y", T.cb[:], T.c0[:], [], "cb", "c0", 2.0)
     dma("S", T.wts[:], T.wt[:], [], "wts", "wt", 2.0)
-    dma("Y", T.hdi[:], T.hd[:], [], "hdi", "hd", 4.0)
+    dma("Y", T.hdi[:], T.hd[:], [], "hdi", "hd", LH)
     dma("S", T.thi[:], T.th[:], [], "thi", "th", 2.0)
-    dma("Y", T.xs[:, 0:V], T.xr[:], [], "x", "xr", 7.0)
-    dma("Y", T.nxs[:, 0:V], T.nx[:], [], "nx", "nx", 12.0)
+    dma("Y", T.nxs[:, 0:V], T.nx[:], [], "nx", "nx", LN)
+    dma("Y", T.xs[:, 0:V], T.xr[:], [], "x", "xr", LX)
     io(co("pc"), "pc", [[0, 1]], 0, 1, 1)
     op("G", 0.16, [], ["pi"], lambda: g.iota(T.pi[:], [[0, 1]], 0, 1))
 
@@ -213,9 +224,8 @@ def declare(g, core, T, topo):
     io(T.m15[:], "m15", [[0, 8], [1, 16]], 0, 0, 128)
     io(T.mf[:], "mf", [[1, 143]], 0, 0, 143)
     io(T.ce[:], "ce", [[1, 64], [0, 16]], 0, 0, 1024)
-    io(T.seli[:], "seli", [[4096, 16], [16, 8], [-4095, 16]], 0, 0, 2048)
-    io(T.mg128[:], "mg128", [[16, 8], [0, 128]], 0, 0, 1024)
     io(T.sq[:], "sq", [[16, 4]], 0, 0, 4)
+    io(T.mg128[:], "mg128", [[16, 8], [0, 128]], 0, 0, 1024)
     pc, pd, pg = co("pc"), co("pd"), co("pg")
     ts(T.xrot[:], "xrot", T.kx[:], ["kx", "pc"], pc, OP.is_equal, 128)
     ts(T.pdi[:], "pdi", T.pi[:], ["pi"], 15, OP.bitwise_and, 1)
@@ -234,7 +244,7 @@ def declare(g, core, T, topo):
     ts(T.hdf[:], "hdf", T.hdi[:], ["hdi"], -2048.0, OP.add, 1024)
     ts(T.rot[:], "rot", T.kt[:], ["kt", "pc"], pc, OP.is_equal, 128, 0.25, OP.mult)
     ts(T.ma[:], "ma", T.m15[:, 0:16], ["m15", "pd"], pd, OP.is_ge, 16)
-    ts(T.mb[:], "mb", T.m15[:, 0:16], ["m15", "pd"], pd, OP.is_equal, 16, 65535.0, OP.mult)
+    ts(T.mb[:], "mb", T.m15[:, 0:16], ["m15", "pd"], pd, OP.is_equal, 16, 131071.0, OP.mult)
     tt(T.ms[:, 0:16], "ms", T.ma[:], T.mb[:], ["ma", "mb"], OP.add, 16)
     ts(co("s0"), "s0", pd, ["pd"], 0.0, OP.is_gt, 1, 2.0 ** -40, OP.max)
     tt(T.ms[:, 15:16], "ms", T.ms[:, 15:16], co("s0"), ["ms", "s0"], OP.mult, 1)
@@ -242,12 +252,11 @@ def declare(g, core, T, topo):
     while w < 512:
         act(T.ms[:, w:2 * w], "ms", T.ms[:, 0:w], ["ms"], w, AF.Copy)
         w *= 2
-    ts(co("sc0"), "sc0", pd, ["pd"], 0.0, OP.is_equal, 1, 2.0 ** 24, OP.mult)
-    ts(co("scl"), "scl", co("sc0"), ["sc0"], 2.0 ** -16, OP.max, 1)
+    ts(co("sc0"), "sc0", pd, ["pd"], 0.0, OP.is_equal, 1, 2.0 ** 23, OP.mult)
+    ts(co("scl"), "scl", co("sc0"), ["sc0"], 2.0 ** -17, OP.max, 1)
     ts(T.exp[:], "exp", T.ce[:], ["ce", "pc"], co("pc", 0, 64), OP.is_equal, 1024)
     ts(co("pg15"), "pg15", pg, ["pg"], 15.0, OP.add, 1)
     ts(T.bigm[:], "bigm", T.mf[:], ["mf", "pg15"], co("pg15"), OP.is_equal, 143)
-    ts(T.sel[:], "sel", T.seli[:], ["seli", "pc"], pc, OP.is_equal, 2048)
     ms(T.nxs[:, V:XE], "nxe", 4096, 8)
     ms(T.xs[:, V:XE], "xe", 512.0, 8)
     ms(T.c512[:], "c512", 512.0, 128)
@@ -257,6 +266,9 @@ def declare(g, core, T, topo):
     ts(T.tr1[:], "tr1", mf, ["mf", "pc"], pc, OP.is_gt, 128, -2.0, OP.mult)
     tt(T.tr2[:], "tr2", T.tr1[:], T.blf[:], ["tr1", "blf"], OP.mult, 128)
     ts(T.idf[:], "idf", mf, ["mf", "pc"], pc, OP.is_equal, 128)
+    ts(T.eqd[:], "eqd", T.m15[:, 0:16], ["m15", "pd"], pd, OP.is_equal, 16)
+    for d in range(16):
+        act(T.sel[:, d * 128:d * 128 + 128], "sel%d" % d, T.idf[:], ["idf", "eqd"], 128, AF.Copy, scale=T.eqd[:, d:d + 1])
     tt(T.tri[:], "tri", T.tr2[:], T.idf[:], ["tr2", "idf"], OP.add, 128)
     ts(T.nb2[:], "nb2", T.blf[:], ["blf"], -2.0, OP.mult, 128)
     ts(T.nbk[:], "nbk", T.blf[:], ["blf"], -4096.0, OP.mult, 128)
@@ -282,6 +294,7 @@ def declare(g, core, T, topo):
         ts(S("xm%d" % h)[64:128, :], "xmc%d" % h, T.m15[64:128, :], ["m15", "pd", dmo], co("pd", 64, 128), OP.is_equal, 128,
            co(dmo, 64, 128), OP.mult)
 
+    setup[0] = False
     for t in range(RO):
         offk, rdk = "off%d" % t, "rdf%d" % t
         off, rdf = S(offk), S(rdk)
@@ -315,12 +328,13 @@ def declare(g, core, T, topo):
                 act(gh[:, q], "gh" + ps, T.hdf[:].indirect(T.hh[:, lq]), ["hdf", "hh" + hs], 512, AF.Copy, c=GA)
                 op("V", vd(512), ["gh" + ps, "ms"], ["sn" + ps],
                    lambda gh=gh, sn=sn, q=q: g.vector.tensor_tensor_scan(sn[:, q], gh[:, q], T.ms[:], 0.0, OP.add, OP.mult))
-            ts(T.ai[:, hq], "ai" + hs, sn[:, 15:1024:16], ["sn" + hs + "p0", "sn" + hs + "p1", "scl"], co("scl"), OP.mult, 64)
-            ts(T.ah[:, hq], "ah" + hs, T.ai[:, hq], ["ai" + hs], 2048.0, OP.add, 64)
+            sns = ["sn" + hs + "p0", "sn" + hs + "p1", "scl"]
+            ts(T.ah[:, hq], "ah" + hs, sn[:, 15:1024:16], sns, co("scl"), OP.mult, 64, 2048.2425, OP.add)
+            ts(T.ai[:, hq], "ai" + hs, sn[:, 15:1024:16], sns, co("scl"), OP.mult, 64)
             gn = S("gn" + hs)
             ts(gn[:], "gn" + hs, T.nxs[:].indirect(T.ah[:, hq]), ["nx", "nxe", "ah" + hs], 2048.0, OP.subtract, 1024, c=GA)
             mc([(T.p4[:, hq], T.sel[:, d * 128:d * 128 + 128], gn[:, d:1024:16], d == 0, d == 15) for d in range(16)],
-               ["sel", "gn" + hs], "B" + hs, ["p4"], 1024)
+               ["sel%d" % d for d in range(16)] + ["gn" + hs], "B" + hs, ["p4"], 1024)
             ts(T.bh[:, hq], "bh" + hs, T.p4[:, hq], ["B" + hs], 2048.0, OP.add, 64, banks=["p4"])
             for l, lv in enumerate("ab"):
                 xg, yy, av = S("xg" + lv + hs), S("yy" + lv + hs), S("av" + lv + hs)
@@ -378,7 +392,7 @@ def declare(g, core, T, topo):
                 g.remote_dma(out_ap=S(cl)[:], in_ap=S(cn)[:], remote_sem=T.sem["arr%d%d" % (t, h)], local_sem=T.sem.sent,
                              pid=pid, routing_id=rid, dma_engine_mask=topo.mask(core, dst))
             op("G", 0.3, [cn], ["snd" + cl], send, sem=("none", 0), name="send" + cl)
-            op(None, 0.0, ["snd" + cl], [cl], None, sem=("arr%d%d" % (t, h), len(topo.engines(core, dst))), lat=2.8, name="recv" + cl)
+            op(None, 0.0, ["snd" + cl], [cl], None, sem=("arr%d%d" % (t, h), len(topo.engines(core, dst))), lat=CL, name="recv" + cl)
             yk = (t * 2 + h) * 4
             act(T.yq[:, yk:yk + 4], "yq%d" % (t // 2), o4, ["O" + hs], 4, AF.Copy, banks=["p4"])
             if h == 1 and t < RO - 1:
@@ -395,7 +409,7 @@ def declare(g, core, T, topo):
             op("P", 0.03 + 512 * CY, ["yq%d" % e, "idf"], ["PY"], lambda py=py, n0=n0, nc=nc: g.tensor.transpose(py, T.yq[:, n0:n0 + nc], T.idf[:]), ["p6"])
             ts(yb[:], "ytb%d" % e, py, ["PY"], 4096.0, OP.min, 128, banks=["p6"])
             for k in range(8):
-                dma("Y", T.yt[k:k + 1, n0 * 16:(n0 + nc) * 16], yb[:, 16 * k:16 * k + 16], ["ytb%d" % e], "yt%d%d" % (e, k), "yt%d%d" % (e + 1, k), 2.0)
+                dma("YS"[e], T.yt[k:k + 1, n0 * 16:(n0 + nc) * 16], yb[:, 16 * k:16 * k + 16], ["ytb%d" % e], "yt%d%d" % (e, k), "yt%d%d" % (e + 1, k), 2.0)
     return ops
 
 
@@ -444,4 +458,4 @@ def rank_program(g, core, T, topo):
         g.wait_ge(T.sem["e" + e], count[e])
     for s in DMAS:
         if s[0] == "y":
-            g.sync.wait_ge(T.sem["d_" + s], 16)
+            (g.scalar if s[:3] == "yt2" else g.sync).wait_ge(T.sem["d_" + s], 16)

from concourse.mybir import dt, AluOpType, AxisListType, ActivationFunctionType
import comms_topo

OP = AluOpType
AF = ActivationFunctionType
V, HB, CH, RO, H = 4096, 1024, 128, 3, 64
XE = V + 8
XW = XE + 4 * H
A, B, NCH = 0.05, 6.0, 2
LH, LX, LN, CL = 3.3, 10.5, 8.0, 2.8
PR = {'gh0p0': 2, 'yya1p1': -4, 'sn1p1': 4, 'avb0p0': -2, 'hh0': 8, 'RT0': -8, 'idf0': 14, 'half0': -4, 'ai1': -8, 'dum0': -8,
      'qm0': -4, 'yo0': -8, 'xgb1p1': -2, 'xm1': -8, 'ua0': 4, 'hh1': 2, 'yyb1p1': 8, 'nb0': -2, 'SDb1': 4, 'ua1': 4, 'blh0': -2,
      'ah1': -2, 'ui0': 2, 'xga0p0': 8, 'pdi0': -4, 'nbk0': -8, 'ah0': -2, 'ms0': 8, 'one0': -8, 'U1': -8, 'ma0': -4, 'xe0': 2,
      'bh1': 14}

SCRATCH = {"dx": ("psum", [128, 1024], "float32")}


def buf(shape, dtype, names, where="sbuf"):
    for n in names.split():
        SCRATCH[n] = (where, shape, dtype)


buf([128, 512], "float32", "p2 p3 p4 p5 p6 p7", "psum")
buf([128, XW], "bfloat16", "xs")
buf([128, HB], "int32", "hdi")
buf([128, HB], "float32", "hdf mg128")
buf([128, XE], "int32", "nxs")
buf([128, 1], "int32", "thi pi pdi")
COLS = "pc pd pg pg15 corr s0 sc0 scl thf dmo0 dmo1 thr0 thr1 dum0 dum1".split()
buf([128, 16], "float32", "cols ma mb eqd")
buf([128, CH], "bfloat16", "cb c512 xrot tri nb2 nbk")
buf([128, 16], "bfloat16", "wts wt2")
buf([128, 128], "float32", "m15 mg kt kx blk4 tr1 tr2 blf idf xm0 xm1 dd yo")
buf([128, 143], "float32", "mf")
buf([64, 1024], "float32", "ce")
buf([128, 4], "float32", "sq qm")
buf([128, 2048], "bfloat16", "sel")
buf([128, 128], "float16", "rot wr blh brow cf cca ccb")
buf([128, 2], "float16", "k4")
buf([128, 2], "float32", "k4f")
buf([128, 143], "bfloat16", "bigm")
buf([64, 64], "float16", "idh")
buf([64, 128], "float16", "far")
buf([128, 1024], "float16", "msk")
buf([64, 1024], "bfloat16", "exp")
buf([128, 512], "float32", "ms")
buf([1, 128], "float32", "half zero pow")
buf([1, 16], "float32", "one")
buf([128, 24], "float32", "yq")
buf([16, 128], "float32", "yt1")
buf([8, 128], "float32", "yt2")
buf([128, 128], "int32", "ui ua ub up uh ai")
buf([128, 128], "uint16", "hh ah bh")
for _h in "01":
    buf([64, 128], "bfloat16", "dt" + _h)
    buf([128, 1024], "float32", "gh" + _h + " sn" + _h)
    buf([128, 1024], "float16", "gn" + _h)
    buf([128, 128], "bfloat16", "near" + _h + " cho" + _h)
    buf([128, 512], "bfloat16", "eq" + _h)
    buf([64, 128], "float32", "win" + _h)
    buf([128, 1024], "bfloat16", " ".join(k + l + _h for k in ("xg", "yy", "av") for l in "ab"))
for _t in range(RO):
    buf([128, 128], "float16", "rdf%d" % _t)
    buf([128, 8], "uint16", "off%d" % _t)
    buf([128, H], "float16", " ".join("%s%d%d" % (k, _t, h) for k in ("cn", "cl") for h in range(2)))
DMAS = ["c0", "wt", "th", "hd", "xr", "nx", "yc0", "yc1"] + ["yt1%d" % k for k in range(8)] + ["yt2%d" % k for k in range(8)]
SEMAPHORES = ["eV", "eS", "eP", "eG", "sent"] + ["arr%d%d" % (t, h) for t in range(RO) for h in range(2)] + ["d_" + k for k in DMAS]

CY, FX, LAT = 0.00095, 0.03, 0.03
GA = 1.56


def schedule(ops):
    n = len(ops)
    succ = [[] for _ in range(n)]
    for o in ops:
        for d in o["deps"]:
            succ[d].append(o["id"])
    prio = [0.0] * n
    for k in range(n - 1, -1, -1):
        prio[k] = ops[k]["dur"] + ops[k]["lat"] + max([prio[s] + LAT for s in succ[k]] or [0.0])
    want = [prio[k] - B * ops[k]["st"] for k in range(n)]
    for k in range(n):
        if ops[k]["set"] and (ops[k]["eng"] == "G" or ops[k]["sem"]):
            want[k] = 1000.0 - k
        else:
            want[k] += PR.get(ops[k]["kind"], 0.0)
    left = [len(o["deps"]) for o in ops]
    ready = {}
    for k in range(n):
        if left[k] == 0:
            ready.setdefault(ops[k]["eng"], []).append(k)
    fin, free, bank, order, begin = [0.0] * n, {}, {}, [], [0.0] * n
    while any(ready.values()):
        pick = None
        for e in ready:
            est = []
            for k in ready[e]:
                o = ops[k]
                s = max([free.get(e, 0.0) if e else 0.0] + [fin[d] + LAT for d in o["deps"]])
                for b in o["banks"]:
                    for x, q in bank.get(b, {}).items():
                        if x != e:
                            s = max(s, fin[q] + LAT)
                est.append((s, k))
            if est:
                t = min(est)[0]
                if pick is None or t < pick[0]:
                    w, k, s = max((want[k], -k, s) for s, k in est if s <= t + A)
                    pick = (t, -k, s)
        t, k, s = pick
        o = ops[k]
        e = o["eng"]
        ready[e].remove(k)
        begin[k] = s
        fin[k] = s + o["dur"] + o["lat"]
        if e:
            free[e] = s + o["dur"]
        for b in o["banks"]:
            q = bank.setdefault(b, {})
            o["bdeps"] += [v for x, v in q.items() if x != e]
            q[e] = k
        order.append(k)
        for x in succ[k]:
            left[x] -= 1
            if left[x] == 0:
                ready.setdefault(ops[x]["eng"], []).append(x)
    return order, begin, fin


def declare(g, core, T, topo):
    rank = T.rank_of(core)
    ops, lastw, readers, stage, setup = [], {}, {}, [0], [True]

    def op(eng, dur, rd, wr, fn, banks=(), sem=None, lat=0.0, name="", strict=False):
        k = len(ops)
        deps, war = set(), set()
        for r in rd + wr:
            if r in lastw:
                deps.add(lastw[r])
        for w in wr:
            for q in readers.get(w, []):
                if ops[q]["eng"] == eng and not ops[q]["sem"] and q not in deps and not strict:
                    war.add(q)
        for w in wr:
            deps |= set(readers.get(w, []))
        for r in rd:
            readers.setdefault(r, []).append(k)
        for w in wr:
            lastw[w] = k
            readers[w] = []
        deps.discard(k)
        name = name or wr[0]
        ops.append({"id": k, "eng": eng, "dur": dur, "lat": lat, "deps": sorted(deps), "bdeps": [], "war": war, "fn": fn,
                    "banks": tuple(banks), "sem": sem, "name": name, "st": stage[0], "set": setup[0],
                    "kind": name.strip("0123456789") + str(stage[0] % 2)})

    def vd(n, c=1.0):
        return FX + max(64, n * c) * CY

    def S(n):
        return T[n]

    def co(n, a=0, b=128):
        j = COLS.index(n)
        return T.cols[a:b, j:j + 1]

    def ts(out, okey, in0, rd, s1, op0, n, s2=None, op1=None, c=1.0, banks=()):
        def fn():
            if op1 is None:
                return g.vector.tensor_scalar(out, in0, s1, None, op0)
            return g.vector.tensor_scalar(out, in0, s1, s2, op0, op1)
        op("V", vd(n, c), rd, [okey], fn, banks)

    def tt(out, okey, in0, in1, rd, o, n, c=2.0, banks=()):
        op("V", vd(n, c), rd, [okey], lambda: g.vector.tensor_tensor(out, in0, in1, o), banks)

    def cp(out, okey, in_, rd, n, banks=()):
        op("V", vd(n), rd, [okey], lambda: g.vector.tensor_copy(out, in_), banks)

    def ms(ap, key, val, n):
        op("V", vd(n), [], [key], lambda: g.vector.memset(ap, val))

    def act(out, okey, in_, rd, n, func, c=1.0, banks=(), **kw):
        op("S", vd(n, c), rd, [okey], lambda: g.scalar.activation(out, in_, func, **kw), banks)

    def io(ap, key, pattern, base, cm, n):
        op("G", 0.16 + 2 * n * CY, [], [key], lambda: g.iota(ap, pattern, base, cm, allow_small_or_imprecise_dtypes=True))

    def mm(calls, rd, wr, banks, cyc):
        def fn():
            for out, l, r, a, z in calls:
                q = g.tensor.matmul(out, l, r, a, z)
            return q
        op("P", 0.03 + cyc * CY, rd, [wr], fn, banks)

    def mc(calls, rd, wr, banks, cyc):
        w = len(calls) // NCH
        for j in range(NCH):
            mm(calls[j * w:j * w + w], rd, wr, banks, cyc / NCH)
            if j:
                ops[-1]["war"].add(ops[-2]["id"])

    def dma(eng, out, in_, rd, wr, sem, lat):
        q = g.sync if eng == "Y" else g.scalar
        op(eng, 0.1, rd, [wr], lambda: q.dma_start(out, in_), sem=("d_" + sem, 16), lat=lat)

    dma("Y", T.cb[:], T.c0[:], [], "cb", "c0", 2.0)
    dma("S", T.wts[:], T.wt[:], [], "wts", "wt", 2.0)
    dma("Y", T.hdi[:], T.hd[:], [], "hdi", "hd", LH)
    dma("S", T.thi[:], T.th[:], [], "thi", "th", 2.0)
    dma("Y", T.nxs[:, 0:V], T.nx[:], [], "nx", "nx", LN)
    dma("Y", T.xs[:, 0:V], T.xr[:], [], "x", "xr", LX)
    io(co("pc"), "pc", [[0, 1]], 0, 1, 1)
    op("G", 0.16, [], ["pi"], lambda: g.iota(T.pi[:], [[0, 1]], 0, 1))

    def iwrap(b, key, base, col, wbase):
        io(b[:], key, [[16, 8], [1, 16]], base, 0, 128)
        op("G", 0.18, [key], [key], lambda: g.iota(b[:, col:128:16], [[16, 8]], wbase, 0, allow_small_or_imprecise_dtypes=True))
    iwrap(T.kx, "kx", -1, 0, 15)
    io(T.mg[:], "mg", [[16, 8], [0, 16]], 0, 0, 128)
    iwrap(T.kt, "kt", 1, 15, 0)
    io(T.m15[:], "m15", [[0, 8], [1, 16]], 0, 0, 128)
    io(T.mf[:], "mf", [[1, 143]], 0, 0, 143)
    io(T.ce[:], "ce", [[1, 64], [0, 16]], 0, 0, 1024)
    io(T.sq[:], "sq", [[16, 4]], 0, 0, 4)
    io(T.mg128[:], "mg128", [[16, 8], [0, 128]], 0, 0, 1024)
    pc, pd, pg = co("pc"), co("pd"), co("pg")
    ts(T.xrot[:], "xrot", T.kx[:], ["kx", "pc"], pc, OP.is_equal, 128)
    ts(T.pdi[:], "pdi", T.pi[:], ["pi"], 15, OP.bitwise_and, 1)
    cp(pd, "pd", T.pdi[:], ["pdi"], 1)
    tt(pg, "pg", pc, pd, ["pc", "pd"], OP.subtract, 1)
    ts(T.blk4[:], "blk4", T.mg[:], ["mg", "pg"], pg, OP.is_equal, 128, 0.25, OP.mult)
    for h in range(2):
        q = slice(h * H, h * H + H)
        ts(T.cf[:, q], "cf%d" % h, T.cb[:, q], ["cb"], 4.0, OP.mult, 64, 5120.0, OP.add)
    mm([(T.p2[:, 384 + 16 * k:400 + 16 * k], T.xrot[:], T.wts[:], True, True) for k in range(8)], ["xrot", "wts"], "RA", ["p2"], 512)
    tt(T.wr[:], "wr", T.p2[:, 384:512], T.blk4[:], ["RA", "blk4"], OP.mult, 128, 1.0, ["p2"])
    ms(T.k4f[:], "k4f", 5120.0, 2)
    cp(T.k4[:], "k4", T.k4f[:], ["k4f"], 2)
    mm([(T.p2[:, 384:386], T.wr[:], T.k4[:], True, True)], ["wr", "k4"], "RA", ["p2"], 64)
    cp(co("corr"), "corr", T.p2[:, 384:385], ["RA"], 1, ["p2"])
    ts(T.hdf[:], "hdf", T.hdi[:], ["hdi"], -2048.0, OP.add, 1024)
    ts(T.rot[:], "rot", T.kt[:], ["kt", "pc"], pc, OP.is_equal, 128, 0.25, OP.mult)
    ts(T.ma[:], "ma", T.m15[:, 0:16], ["m15", "pd"], pd, OP.is_ge, 16)
    ts(T.mb[:], "mb", T.m15[:, 0:16], ["m15", "pd"], pd, OP.is_equal, 16, 131071.0, OP.mult)
    tt(T.ms[:, 0:16], "ms", T.ma[:], T.mb[:], ["ma", "mb"], OP.add, 16)
    ts(co("s0"), "s0", pd, ["pd"], 0.0, OP.is_gt, 1, 2.0 ** -40, OP.max)
    tt(T.ms[:, 15:16], "ms", T.ms[:, 15:16], co("s0"), ["ms", "s0"], OP.mult, 1)
    w = 16
    while w < 512:
        act(T.ms[:, w:2 * w], "ms", T.ms[:, 0:w], ["ms"], w, AF.Copy)
        w *= 2
    ts(co("sc0"), "sc0", pd, ["pd"], 0.0, OP.is_equal, 1, 2.0 ** 23, OP.mult)
    ts(co("scl"), "scl", co("sc0"), ["sc0"], 2.0 ** -17, OP.max, 1)
    ts(T.exp[:], "exp", T.ce[:], ["ce", "pc"], co("pc", 0, 64), OP.is_equal, 1024)
    ts(co("pg15"), "pg15", pg, ["pg"], 15.0, OP.add, 1)
    ts(T.bigm[:], "bigm", T.mf[:], ["mf", "pg15"], co("pg15"), OP.is_equal, 143)
    ms(T.nxs[:, V:XE], "nxe", 4096, 8)
    ms(T.xs[:, V:XE], "xe", 512.0, 8)
    ms(T.c512[:], "c512", 512.0, 128)
    cp(co("thf"), "thf", T.thi[:], ["thi"], 1)
    mf = T.mf[:, 0:128]
    ts(T.blf[:], "blf", T.mg[:], ["mg", "pg"], pg, OP.is_equal, 128)
    ts(T.tr1[:], "tr1", mf, ["mf", "pc"], pc, OP.is_gt, 128, -2.0, OP.mult)
    tt(T.tr2[:], "tr2", T.tr1[:], T.blf[:], ["tr1", "blf"], OP.mult, 128)
    ts(T.idf[:], "idf", mf, ["mf", "pc"], pc, OP.is_equal, 128)
    ts(T.eqd[:], "eqd", T.m15[:, 0:16], ["m15", "pd"], pd, OP.is_equal, 16)
    for d in range(16):
        act(T.sel[:, d * 128:d * 128 + 128], "sel%d" % d, T.idf[:], ["idf", "eqd"], 128, AF.Copy, scale=T.eqd[:, d:d + 1])
    tt(T.tri[:], "tri", T.tr2[:], T.idf[:], ["tr2", "idf"], OP.add, 128)
    ts(T.nb2[:], "nb2", T.blf[:], ["blf"], -2.0, OP.mult, 128)
    ts(T.nbk[:], "nbk", T.blf[:], ["blf"], -4096.0, OP.mult, 128)
    cp(T.blh[:], "blh", T.blf[:], ["blf"], 128)
    ts(T.msk[:], "msk", T.mg128[:], ["mg128", "pc"], pc, OP.is_equal, 1024)
    ts(T.brow[:], "brow", T.mg[:], ["mg", "pc"], pc, OP.is_equal, 128)
    cp(T.idh[:], "idh", T.idf[0:64, 0:64], ["idf"], 64)
    ts(T.far[:], "far", T.m15[0:64, :], ["m15", "pd"], co("pd", 0, 64), OP.not_equal, 128, 16384.0, OP.mult)
    ts(T.qm[0:64, :], "qm0", T.sq[0:64, :], ["sq", "pg"], co("pg", 0, 64), OP.is_equal, 4)
    ts(T.qm[64:128, :], "qm1", T.sq[64:128, :], ["sq", "pg"], 64.0, OP.add, 4, co("pg", 64, 128), OP.is_equal)
    ms(T.half[:], "half", 0.5, 128)
    ms(T.zero[:], "zero", 0.0, 128)
    ms(T.one[:], "one", 1.0, 16)
    op("V", vd(128), ["half", "zero"], ["pow"], lambda: g.vector.tensor_tensor_scan(T.pow[:], T.half[:], T.zero[:], 2.0 ** 64, OP.mult, OP.add))
    mm([(T.p7[:, 0:16], T.pow[:], T.one[:], True, True)], ["pow", "one"], "R0", ["p7"], 256)
    cp(T.wt2[:], "wt2", T.p7[:, 0:16], ["R0"], 16, ["p7"])
    ts(co("thr0", 0, 64), "thr0", T.p7[0:64, 0:1], ["R0"], 2.5, OP.mult, 1, banks=["p7"])
    ts(co("thr1", 0, 64), "thr1", co("thr0", 0, 64), ["thr0"], 2.0 ** -64, OP.mult, 1)
    for h in range(2):
        dum, dmo = "dum%d" % h, "dmo%d" % h
        ts(co(dum, 0, 64), dum, co("pc", 0, 64), ["pc"], 2.0, OP.mult, 1, float(XE - 2048 + 2 * H * h), OP.add)
        ts(co(dmo), dmo, pc, ["pc"], 2.0, OP.mult, 1, float(XE + 2 * H * h - 128), OP.add)
        ts(S("xm%d" % h)[64:128, :], "xmc%d" % h, T.m15[64:128, :], ["m15", "pd", dmo], co("pd", 64, 128), OP.is_equal, 128,
           co(dmo, 64, 128), OP.mult)

    setup[0] = False
    for t in range(RO):
        offk, rdk = "off%d" % t, "rdf%d" % t
        off, rdf = S(offk), S(rdk)
        for h in range(2):
            hs = str(h)
            hq = slice(h * H, h * H + H)
            stage[0] = 2 * t + h
            ck = "cf" + hs if t == 0 else "cl%d%s" % (t - 1, hs)

            def chain():
                return T.cf[:, hq] if t == 0 else S(ck)[:]
            mm([(T.p2[:, hq], T.wr[:], chain(), True, True)], ["wr", ck], "U" + hs, ["p2"], 64)
            mm([(T.p3[:, 0:64], T.rot[:], chain(), True, True)], ["rot", ck], "D", ["p3"], 64)
            mm([(T.p3[0:64, 128:256], chain(), T.rot[:], True, True)], ["rot", ck], "DT", ["p3"], 128)
            ts(T.ui[:, hq], "ui" + hs, T.p2[:, hq], ["U" + hs, "corr"], co("corr"), OP.subtract, 64, banks=["p2"])
            ts(T.ua[:, hq], "ua" + hs, T.ui[:, hq], ["ui" + hs], 4095, OP.bitwise_and, 64)
            ts(T.ub[:, hq], "ub" + hs, T.ua[:, hq], ["ua" + hs], 32.0, OP.add, 64)
            tt(T.up[:, hq], "up" + hs, T.ua[:, hq], T.ub[:, hq], ["ua" + hs, "ub" + hs], OP.mult, 64)
            ts(T.uh[:, hq], "uh" + hs, T.up[:, hq], ["up" + hs], 5, OP.logical_shift_right, 64, 1023, OP.bitwise_and)
            cp(T.hh[:, hq], "hh" + hs, T.uh[:, hq], ["uh" + hs], 64)
            act(S("dt" + hs)[:], "dt" + hs, T.p3[0:64, 128:256], ["DT"], 128, AF.Identity, banks=["p3"], bias=-1280.0)
            act(T.dd[:, hq], "dd" + hs, T.p3[:, 0:64], ["D"], 64, AF.Identity, banks=["p3"], bias=1278.5, scale=3.0)
            lo = XE + 2 * H * h
            act(T.xs[:, lo:lo + 2 * H:2], "xd" + hs, T.p3[:, 0:64], ["D"], 64, AF.Identity, banks=["p3"], bias=-1280.0)
            for p in range(2):
                q = slice(p * 512, p * 512 + 512)
                mm([(T.dx[:, q], S("dt" + hs)[:], T.exp[:, q], True, True)], ["dt" + hs, "exp"], "DX%d" % p, ["x%d" % p], 512)
            gh, sn = S("gh" + hs), S("sn" + hs)
            for p in range(2):
                q, ps, lq = slice(p * 512, p * 512 + 512), hs + "p%d" % p, slice(h * H + p * 32, h * H + p * 32 + 32)
                act(gh[:, q], "gh" + ps, T.hdf[:].indirect(T.hh[:, lq]), ["hdf", "hh" + hs], 512, AF.Copy, c=GA)
                op("V", vd(512), ["gh" + ps, "ms"], ["sn" + ps],
                   lambda gh=gh, sn=sn, q=q: g.vector.tensor_tensor_scan(sn[:, q], gh[:, q], T.ms[:], 0.0, OP.add, OP.mult))
            sns = ["sn" + hs + "p0", "sn" + hs + "p1", "scl"]
            ts(T.ah[:, hq], "ah" + hs, sn[:, 15:1024:16], sns, co("scl"), OP.mult, 64, 2048.2425, OP.add)
            ts(T.ai[:, hq], "ai" + hs, sn[:, 15:1024:16], sns, co("scl"), OP.mult, 64)
            gn = S("gn" + hs)
            ts(gn[:], "gn" + hs, T.nxs[:].indirect(T.ah[:, hq]), ["nx", "nxe", "ah" + hs], 2048.0, OP.subtract, 1024, c=GA)
            mc([(T.p4[:, hq], T.sel[:, d * 128:d * 128 + 128], gn[:, d:1024:16], d == 0, d == 15) for d in range(16)],
               ["sel%d" % d for d in range(16)] + ["gn" + hs], "B" + hs, ["p4"], 1024)
            ts(T.bh[:, hq], "bh" + hs, T.p4[:, hq], ["B" + hs], 2048.0, OP.add, 64, banks=["p4"])
            for l, lv in enumerate("ab"):
                xg, yy, av = S("xg" + lv + hs), S("yy" + lv + hs), S("av" + lv + hs)
                for p in range(2):
                    q, ps, lq = slice(p * 512, p * 512 + 512), lv + hs + "p%d" % p, slice(h * H + p * 32, h * H + p * 32 + 32)
                    act(xg[:, q], "xg" + ps, T.xs[:, 0:XE].indirect(S(lv + "h")[:, lq]), ["x", "xe", lv + "h" + hs], 512, AF.Copy, c=GA)
                    tt(yy[:, q], "yy" + ps, xg[:, q], T.dx[:, q], ["xg" + ps, "DX%d" % p], OP.subtract, 512, 1.0, ["x%d" % p])
                    act(av[:, q], "av" + ps, yy[:, q], ["yy" + ps], 512, AF.Abs)
                z = h * 128 + l * 64
                mc([(T.p5[:, z:z + 64], T.bigm[:, 15 - d:143 - d], av[:, d:1024:16], d == 0, d == 15)
                    for d in range(16)], ["bigm", "av" + lv + hs + "p0", "av" + lv + hs + "p1"], "SD" + lv + hs, ["p5"], 1024)
            nr, cho = S("near" + hs), S("cho" + hs)
            ts(nr[:], "near" + hs, T.p5[:, h * 128:h * 128 + 128], ["SDa" + hs, "SDb" + hs, "thf"], co("thf"), OP.is_le, 128, banks=["p5"])
            z = 256 + h * 128
            mm([(T.p3[:, z:z + 64], T.tri[:], nr[:, 0:64], True, True), (T.p3[:, z + 64:z + 128], T.tri[:], nr[:, 64:128], True, False),
                (T.p3[:, z + 64:z + 128], T.nb2[:], nr[:, 0:64], False, True)], ["tri", "nb2", "near" + hs], "Z" + hs, ["p3"], 192)
            act(cho[:], "cho" + hs, T.p3[:, z:z + 128], ["Z" + hs], 128, AF.Relu, banks=["p3"])
            tt(T.cca[:, hq], "cca" + hs, cho[:, 0:64], T.ai[:, hq], ["cho" + hs, "ai" + hs], OP.mult, 64)
            tt(T.ccb[:, hq], "ccb" + hs, cho[:, 64:128], T.p4[:, hq], ["cho" + hs, "B" + hs], OP.mult, 64, 1.0, ["p4"])
            rb = T.p6[:, hq]
            mm([(rb, T.nbk[:], cho[:, 0:64], True, False), (rb, T.nbk[:], cho[:, 64:128], False, False),
                (rb, T.blh[:], T.cca[:, hq], False, False), (rb, T.blh[:], T.ccb[:, hq], False, True)],
               ["nbk", "blh", "cho" + hs, "cca" + hs, "ccb" + hs], "RB" + hs, ["p6"], 256)
            ts(rdf[:, hq], rdk + hs, rb, ["RB" + hs], 4096.0, OP.add, 64, banks=["p6"])
            m = 64 * (h + 1)
            low = [rdk + "0", rdk + "1"][:h + 1]
            mm([(T.p6[0:m, 256:384], rdf[:, 0:m], T.brow[:], True, True)], ["brow"] + low, "RC", ["p6"], 128)
            eq = S("eq" + hs)
            for b in range(2):
                mm([(T.p7[0:m, j * 64:j * 64 + 64], T.msk[:, j * 128:j * 128 + m], rdf[:, hq], True, True) for j in range(4 * b, 4 * b + 4)],
                   ["msk", rdk + hs], "R%d" % b, ["p7"], 256)
            rt = T.p6[0:64, 384:512]
            mm([(rt, rdf[:, hq], T.brow[:], True, False), (rt, T.idh[:], T.far[:], False, True)], [rdk + hs, "brow", "idh", "far"],
               "RT", ["p6"], 256)
            for b in range(2):
                for j in range(4 * b, 4 * b + 4):
                    ts(eq[0:m, j * 64:j * 64 + 64], "eq%s%d" % (hs, j), T.p7[0:m, j * 64:j * 64 + 64], ["R%d" % b, "RC"],
                       T.p6[0:m, 256 + 16 * j:257 + 16 * j], OP.is_equal, 64, banks=["p7", "p6"])
                mm([(T.p2[0:64, 128 + 16 * j:144 + 16 * j], eq[0:m, j * 64:j * 64 + 64], T.wt2[0:m, :], True, True) for j in range(4 * b, 4 * b + 4)],
                   ["eq%s%d" % (hs, j) for j in range(4 * b, 4 * b + 4)] + ["wt2"], "L%d" % b, ["p2"], 256)
            ts(rt, "RT", rt, ["RT", "dum" + hs], co("dum" + hs, 0, 64), OP.subtract, 128, 0.0, OP.min, banks=["p6"])
            ts(S("win" + hs)[:], "win" + hs, T.p2[0:64, 128:256], ["L0", "L1", "thr" + hs], co("thr" + hs, 0, 64), OP.is_lt, 128, banks=["p2"])
            xm = S("xm" + hs)
            tt(xm[0:64, :], "xm" + hs, S("win" + hs)[:], rt, ["win" + hs, "RT"], OP.mult, 128, 1.0, ["p6"])
            o4 = T.p4[:, 128 + 4 * h:132 + 4 * h]
            mm([(o4, xm[:], T.qm[:], True, True)], ["xm" + hs, "xmc" + hs, "qm0", "qm1"], "O" + hs, ["p4"], 256)
            cp(off[:, h * 4:h * 4 + 4], offk + hs, o4, ["O" + hs], 4, ["p4"])
            cn, cl = "cn%d%s" % (t, hs), "cl%d%s" % (t, hs)
            tt(S(cn)[:], cn, T.xs[:].indirect(off[:, h * 4:h * 4 + 4]), T.dd[:, hq],
               ["x", "xe", "xd0", "xd1", offk + hs, "dd" + hs], OP.add, 64, GA)
            dst = T.cores[(rank + 1 + t % 3) % 4]

            def send(dst=dst, cn=cn, cl=cl, t=t, h=h):
                rid, pid = topo.addr(dst)[0:2]
                g.remote_dma(out_ap=S(cl)[:], in_ap=S(cn)[:], remote_sem=T.sem["arr%d%d" % (t, h)], local_sem=T.sem.sent,
                             pid=pid, routing_id=rid, dma_engine_mask=topo.mask(core, dst))
            op("G", 0.3, [cn], ["snd" + cl], send, sem=("none", 0), name="send" + cl)
            op(None, 0.0, ["snd" + cl], [cl], None, sem=("arr%d%d" % (t, h), len(topo.engines(core, dst))), lat=CL, name="recv" + cl)
            yk = (t * 2 + h) * 4
            act(T.yq[:, yk:yk + 4], "yq%d" % (t // 2), o4, ["O" + hs], 4, AF.Copy, banks=["p4"])
            if h == 1 and t < RO - 1:
                op("V", FX + 128 * 3.5 * CY, [offk + "0", offk + "1", "c512"], ["x", "xe", "xd0", "xd1"],
                   lambda off=off: g.vector.tensor_copy(T.xs[:].indirect(off[:, 0:8]), T.c512[:]), name="scatter", strict=True)
            if t == RO - 1:
                ts(T.yo[:, hq], "yo" + hs, S(cl)[:], [cl], 0.25, OP.mult, 64, -1280.0, OP.add)
                dma("Y", T.yc[:, hq], T.yo[:, hq], ["yo" + hs], "out" + hs, "yc%d" % h, 2.0)
        if t >= 1:
            e = t - 1
            n0, nc = (0, 16) if e == 0 else (16, 8)
            yb = S("yt%d" % (e + 1))
            py = T.p6[0:nc, 128:256]
            op("P", 0.03 + 512 * CY, ["yq%d" % e, "idf"], ["PY"], lambda py=py, n0=n0, nc=nc: g.tensor.transpose(py, T.yq[:, n0:n0 + nc], T.idf[:]), ["p6"])
            ts(yb[:], "ytb%d" % e, py, ["PY"], 4096.0, OP.min, 128, banks=["p6"])
            for k in range(8):
                dma("YS"[e], T.yt[k:k + 1, n0 * 16:(n0 + nc) * 16], yb[:, 16 * k:16 * k + 16], ["ytb%d" % e], "yt%d%d" % (e, k), "yt%d%d" % (e + 1, k), 2.0)
    return ops


def rank_program(g, core, T, topo):
    if T.rank_of(core) is None:
        return
    ops = declare(g, core, T, topo)
    order = schedule(ops)[0]
    queue = {"V": g.vector, "S": g.scalar, "P": g.tensor, "G": g, "Y": g.sync}
    count = {"V": 0, "S": 0, "P": 0, "G": 0}
    known = {e: {} for e in queue}
    done = [None] * len(ops)
    for k in order:
        o = ops[k]
        e = o["eng"]
        if e is None:
            done[k] = (o["sem"][0], o["sem"][1], {})
            continue
        need = {}
        for d in (set(o["deps"]) - o["war"]) | set(o["bdeps"]):
            s, v, kn = done[d]
            if s == "none":
                continue
            if known[e].get(s, 0) < v and (s not in need or need[s][0] < v):
                need[s] = (v, kn)
        for s in sorted(need):
            if not any(q != s and need[q][1].get(s, 0) >= need[s][0] for q in need):
                queue[e].wait_ge(T.sem[s], need[s][0])
        for s in need:
            v, kn = need[s]
            known[e][s] = max(known[e].get(s, 0), v)
            for q, x in kn.items():
                known[e][q] = max(known[e].get(q, 0), x)
        ins = o["fn"]()
        if o["sem"] is None:
            count[e] += 1
            ins.then_inc(T.sem["e" + e], 1)
            done[k] = ("e" + e, count[e], dict(known[e]))
        elif o["sem"][0] == "none":
            done[k] = ("none", 0, {})
        else:
            ins.then_inc(T.sem[o["sem"][0]], o["sem"][1])
            done[k] = (o["sem"][0], o["sem"][1], dict(known[e]))
    g.wait_ge(T.sem.sent, sum(o["sem"][1] for o in ops if o["eng"] is None))
    for e in sorted(count):
        g.wait_ge(T.sem["e" + e], count[e])
    for s in DMAS:
        if s[0] == "y":
            (g.scalar if s[:3] == "yt2" else g.sync).wait_ge(T.sem["d_" + s], 16)
